import numpy as np
CORES = [2,10,18,26,34,42,50,58,66,74,82,90,98,106,114,122,130,138,146,154,162,170,178,186,194,202,210,218,226,234,242,250]
N = 32
H = 2
PERIODIC = True
def setup_inputs(rng):
    return {"x": rng.standard_normal((N, 128, 64), dtype=np.float32)}
def reference(x):
    W = x.shape[2]
    y = np.zeros((N, 128, W + 2 * H), x.dtype)
    for r in range(N):
        y[r][:, H:H + W] = x[r]
        left, right = r - 1, r + 1
        if PERIODIC:
            left, right = left % N, right % N
        if 0 <= left < N:
            y[r][:, :H] = x[left][:, W - H:]
        if 0 <= right < N:
            y[r][:, W + H:] = x[right][:, :H]
    return {"y": y}

@@ -1,0 +1,37 @@
+from concourse.bass import DstId, RemoteDMATransfer
+
+H = 2
+W = 64
+
+SCRATCH = {
+    "buf": ("sbuf", [128, W + 2 * H], "float32"),
+}
+SEMAPHORES = ["loaded", "arrived", "stored"]
+
+
+def rank_program(g, core, T, topo):
+    rank = T.rank_of(core)
+    if rank is None:
+        return
+    n = len(T.cores)
+    left, right = T.cores[(rank - 1) % n], T.cores[(rank + 1) % n]
+    buf = T.buf
+
+    g.dma_start(buf[:, H:H + W], T.x[:, :]).then_inc(T.sem.loaded, 16)
+    g.wait_ge(T.sem.loaded, 16)
+
+    lr, lp = topo.addr(left, core)
+    rr, rp = topo.addr(right, core)
+    g.remote_dma_fused(
+        [
+            RemoteDMATransfer(dst_ids=[DstId(rid=lr, pnc=lp)], dma_engine_mask=0x0F, remote_sem=T.sem.arrived,
+                              src=buf[:, H:2 * H], dst=buf[:, H + W:2 * H + W]),
+            RemoteDMATransfer(dst_ids=[DstId(rid=rr, pnc=rp)], dma_engine_mask=0xF0, remote_sem=T.sem.arrived,
+                              src=buf[:, W:H + W], dst=buf[:, 0:H]),
+        ],
+        local_sem=T.sem.arrived,
+    )
+    g.wait_ge(T.sem.arrived, 16)
+
+    g.dma_start(T.y[:, :], buf[:, :]).then_inc(T.sem.stored, 16)
+    g.wait_ge(T.sem.stored, 16)

@@ -1,5 +1,3 @@
-from concourse.bass import DstId, RemoteDMATransfer
-
 H = 2
 W = 64
 
@@ -20,18 +18,15 @@ def rank_program(g, core, T, topo):
     g.dma_start(buf[:, H:H + W], T.x[:, :]).then_inc(T.sem.loaded, 16)
     g.wait_ge(T.sem.loaded, 16)
 
-    lr, lp = topo.addr(left, core)
-    rr, rp = topo.addr(right, core)
-    g.remote_dma_fused(
-        [
-            RemoteDMATransfer(dst_ids=[DstId(rid=lr, pnc=lp)], dma_engine_mask=0x0F, remote_sem=T.sem.arrived,
-                              src=buf[:, H:2 * H], dst=buf[:, H + W:2 * H + W]),
-            RemoteDMATransfer(dst_ids=[DstId(rid=rr, pnc=rp)], dma_engine_mask=0xF0, remote_sem=T.sem.arrived,
-                              src=buf[:, W:H + W], dst=buf[:, 0:H]),
-        ],
-        local_sem=T.sem.arrived,
-    )
-    g.wait_ge(T.sem.arrived, 16)
+    sends = [
+        (left, buf[:, H:2 * H], buf[:, H + W:2 * H + W]),
+        (right, buf[:, W:H + W], buf[:, 0:H]),
+    ]
+    sends.sort(key=lambda s: topo.mates(core, s[0]))
+    for dst, src_ap, dst_ap in sends:
+        rid, pid = topo.addr(dst, core)
+        g.remote_dma(dst_ap, src_ap, T.sem.arrived, T.sem.arrived, pid, rid, 0xFF)
+    g.wait_ge(T.sem.arrived, 32)
 
     g.dma_start(T.y[:, :], buf[:, :]).then_inc(T.sem.stored, 16)
     g.wait_ge(T.sem.stored, 16)

H = 2
W = 64

SCRATCH = {
    "buf": ("sbuf", [128, W + 2 * H], "float32"),
}
SEMAPHORES = ["loaded", "arrived", "stored"]


def rank_program(g, core, T, topo):
    rank = T.rank_of(core)
    if rank is None:
        return
    n = len(T.cores)
    left, right = T.cores[(rank - 1) % n], T.cores[(rank + 1) % n]
    buf = T.buf

    g.dma_start(buf[:, H:H + W], T.x[:, :]).then_inc(T.sem.loaded, 16)
    g.wait_ge(T.sem.loaded, 16)

    sends = [
        (left, buf[:, H:2 * H], buf[:, H + W:2 * H + W]),
        (right, buf[:, W:H + W], buf[:, 0:H]),
    ]
    sends.sort(key=lambda s: topo.mates(core, s[0]))
    for dst, src_ap, dst_ap in sends:
        rid, pid = topo.addr(dst, core)
        g.remote_dma(dst_ap, src_ap, T.sem.arrived, T.sem.arrived, pid, rid, 0xFF)
    g.wait_ge(T.sem.arrived, 32)

    g.dma_start(T.y[:, :], buf[:, :]).then_inc(T.sem.stored, 16)
    g.wait_ge(T.sem.stored, 16)
